import numpy as np
import ml_dtypes


def mxq(x, axis, fmt="e4m3"):
    dtype, down = {"e4m3": (ml_dtypes.float8_e4m3fn, 7), "e5m2": (ml_dtypes.float8_e5m2, 14)}[fmt]
    v = np.moveaxis(np.asarray(x, np.float32).astype(ml_dtypes.bfloat16).astype(np.float64), axis, -1)
    blocks = v.reshape(v.shape[:-1] + (-1, 32))
    amax = np.abs(blocks).max(-1, keepdims=True)
    byte = np.maximum(np.where(amax > 0, np.frexp(amax)[1] - 1 + 127, 0) - down, 1)
    scale = np.exp2(byte - 127.0)
    codes = (blocks / scale).astype(np.float32).astype(dtype).astype(np.float64)
    return np.moveaxis((codes * scale).reshape(v.shape), -1, axis)


WIDE = False


def mx_kscale(k):
    if not WIDE:
        return np.ones(k)
    levels = np.array([10, -10, 5, -5, 0])
    if k % 512:
        return np.exp2(np.random.permutation(np.resize(levels, k // 32))).repeat(32)
    a = np.empty((k // 512, 16))
    for p in range(k // 512):
        a[p, :8] = np.random.permutation(np.resize(levels, 8))
        for g in range(8):
            far = levels[np.abs(levels - a[p, g]) >= 10]
            a[p, g + 8] = far[np.random.randint(len(far))]
    return np.exp2(a.ravel()).repeat(32)


def f64(x):
    return np.asarray(x).astype(np.float64)


def striped(idx):
    return np.tile(idx.reshape(-1, 16).T, (8, 1)).astype(np.uint16)


def unstriped(offs):
    return offs[:16].T.reshape(-1).astype(np.int64)


def pack_weight(w):
    k, n = w.shape
    w = f64(np.asarray(w, np.float32).astype(ml_dtypes.bfloat16)).reshape(k // 32, 32, n)
    amax = np.abs(w).max(1)
    byte = np.clip(np.where(amax > 0, np.frexp(amax)[1] - 1 + 127 - 7, 1), 1, 254)
    scaled = (w * np.exp2(127.0 - byte)[:, None, :]).reshape(k, n).astype(np.float32)
    words = np.ascontiguousarray(scaled.reshape(k // 512, 128, 4, n).transpose(0, 1, 3, 2)).astype(ml_dtypes.float8_e4m3fn).view(np.uint8)
    return words, np.ascontiguousarray(byte.astype(np.uint8).reshape(k // 512, 16, n))


def unpack_weight(words, scales):
    g, p, n, _ = words.shape
    vals = np.ascontiguousarray(words).view(ml_dtypes.float8_e4m3fn).astype(np.float64) * np.repeat(np.exp2(scales.astype(np.float64) - 127.0), 8, axis=1)[..., None]
    return vals.transpose(0, 1, 3, 2).reshape(g * 512, n)


K, T, D, S, V, N = 1536, 512, 6, 1536, 256, 128


def setup_inputs():
    n = np.random.standard_normal
    s = mx_kscale(K)[:, None]
    words, scales = pack_weight(n((K, N)) / np.sqrt(K) / s)
    return {
        "xT": (n((K, T)) * s).astype(np.float32),
        "w_words": words,
        "w_scales": scales,
        "b": (0.3 * n((N, 1))).astype(np.float32),
        "gate": np.tile(np.random.uniform(0.2, 1.0, (D, 1, V)) / np.sqrt(D), (1, N, 1)).astype(np.float32),
        "pos1": striped(np.random.permutation(T)[:V]),
        "pos2": striped(np.random.permutation(T)[:V]),
        "pos3": striped(np.random.permutation(T)[:V]),
        "pos4": striped(np.random.permutation(T)[:V]),
        "pos5": striped(np.random.permutation(T)[:V]),
        "pos6": striped(np.random.permutation(T)[:V]),
    }


def reference(xT, w_words, w_scales, b, gate, pos1, pos2, pos3, pos4, pos5, pos6):
    w = unpack_weight(w_words, w_scales)
    y = w.T @ mxq(f64(xT), 0, "e4m3")
    y = y + f64(b)
    return sum(f64(gate[d]) * y[:, unstriped(p)] for d, p in enumerate((pos1, pos2, pos3, pos4, pos5, pos6)))

@@ -1,0 +1,131 @@
+from contextlib import ExitStack
+
+import concourse.mybir as mybir
+
+K, T, N, V, D = 1536, 512, 128, 256, 6
+FLOPS = 2 * K * T * N + 2 * D * N * V + T * N
+
+F32 = mybir.dt.float32
+BF16 = mybir.dt.bfloat16
+I32 = mybir.dt.int32
+U32 = mybir.dt.uint32
+U16 = mybir.dt.uint16
+U8 = mybir.dt.uint8
+FP8X4 = mybir.dt.float8_e4m3fn_x4
+IDENTITY = mybir.ActivationFunctionType.Identity
+MULT = mybir.AluOpType.mult
+
+P = 128
+PACK = 4
+K_PASS = P * PACK
+PASSES = K // K_PASS
+H = T // 2
+
+
+def tile_picked_agg_lin_bias_sub_l_kernel(tc, xT, w_words, w_scales, b, gate, pos1, pos2, pos3, pos4, pos5, pos6, out):
+    nc = tc.nc
+    with ExitStack() as ctx:
+        lists = ctx.enter_context(tc.tile_pool(name="lists", bufs=1))
+        keep = ctx.enter_context(tc.tile_pool(name="keep", bufs=1))
+        psum = ctx.enter_context(tc.psum_pool(name="psum", bufs=1))
+
+        offs = [lists.tile([P, V // 16], U16, name="offs%d" % d) for d in range(D)]
+        bias = keep.tile([P, 1], F32)
+        w_codes = keep.tile([P, PASSES, N], U32, align_bytes=64)
+        w_planes = keep.tile([P, PASSES, N], U8, align_bytes=64)
+        warm = keep.tile([P, 2], F32)
+        gates = keep.tile([P, D, V], F32)
+        x_codes = keep.tile([P, PASSES, T], U32, align_bytes=64)
+        x_scales = keep.tile([P, PASSES, T], U8, align_bytes=64)
+        y = keep.tile([P, T], F32)
+
+        chunks = [(0, 0, T), (1, 0, T), (2, 0, H + P), (2, H + P, T)]
+        raws = [keep.tile([P, PACK, c1 - c0], F32, name="raw%d" % i) for i, (a, c0, c1) in enumerate(chunks)]
+        grouped = [keep.tile([P, c1 - c0, PACK], BF16, name="grouped%d" % i, align_bytes=64) for i, (a, c0, c1) in enumerate(chunks)]
+
+        def load(i):
+            a, c0, c1 = chunks[i]
+            nc.sync.dma_start(out=raws[i][:], in_=xT[a * K_PASS : (a + 1) * K_PASS, c0:c1].rearrange("(p j) t -> p j t", j=PACK))
+
+        for q in range(4):
+            nc.scalar.dma_start(out=w_planes[32 * q : 32 * q + 4, :, :].bitcast(I32), in_=w_scales[:, 4 * q : 4 * q + 4, :].rearrange("a q m -> q a m").bitcast(I32))
+        nc.scalar.dma_start(out=bias[:], in_=b)
+        load(0)
+        nc.sync.dma_start(out=w_codes[:].rearrange("p a m -> p (a m)").bitcast(I32).rearrange("p (a m) -> p a m", a=PASSES), in_=w_words.rearrange("a p m r -> p a (m r)").bitcast(I32))
+        load(1)
+        load(2)
+        load(3)
+        poss = (pos1, pos2, pos3, pos4, pos5, pos6)
+        nc.sync.dma_start(offs[0][:], poss[0])
+        nc.sync.dma_start(out=gates[:, 0:2, :], in_=gate[0:2].rearrange("d p v -> p d v"))
+        nc.sync.dma_start(offs[1][:], poss[1])
+        nc.sync.dma_start(out=gates[:, 2:6, :], in_=gate[2:6].rearrange("d p v -> p d v"))
+        for d in range(2, 6):
+            nc.sync.dma_start(offs[d][:], poss[d])
+        nc.vector.memset(warm[:], 0.0)
+        nc.scalar.activation(warm[:, 0:1], warm[:, 1:2], IDENTITY)
+
+        def interleave(copy, i, t0, t1):
+            c0 = chunks[i][1]
+            copy(out=grouped[i][:, t0 - c0 : t1 - c0, :], in_=raws[i][:, :, t0 - c0 : t1 - c0].rearrange("p j t -> p t j"))
+
+        def quantize(i, t0, t1):
+            a, c0, c1 = chunks[i]
+            nc.vector.quantize_mx(
+                out=x_codes[:, a, t0:t1].bitcast(FP8X4),
+                scales=x_scales[:, a, t0:t1],
+                in_=grouped[i][:, t0 - c0 : t1 - c0, :].rearrange("p t j -> p (t j)"),
+            )
+
+        groups = [(0, H), (H, H + P), (H + P, T)]
+        sums = [psum.tile([P, t1 - t0], F32, name="sums%d" % g) for g, (t0, t1) in enumerate(groups)]
+
+        def multiply(a, g):
+            t0, t1 = groups[g]
+            nc.tensor.matmul_mx(
+                out=sums[g][:],
+                lhsT=w_codes[:, a, :].bitcast(FP8X4),
+                lhsT_scale=w_planes[:, a, :],
+                rhs=x_codes[:, a, t0:t1].bitcast(FP8X4),
+                rhs_scale=x_scales[:, a, t0:t1],
+                start=(a == 0),
+                stop=(a == PASSES - 1),
+            )
+
+        for a in range(2):
+            interleave(nc.scalar.copy, a, H, T)
+            interleave(nc.vector.tensor_copy, a, 0, H)
+            quantize(a, 0, H)
+            quantize(a, H, T)
+            for g in range(3):
+                multiply(a, g)
+        interleave(nc.scalar.copy, 2, H, H + P)
+        interleave(nc.vector.tensor_copy, 2, 0, H)
+        quantize(2, 0, H)
+        quantize(2, H, H + P)
+        multiply(2, 0)
+        multiply(2, 1)
+        interleave(nc.scalar.copy, 3, T - 48, T)
+        interleave(nc.vector.tensor_copy, 3, H + P, T - 48)
+        quantize(3, H + P, T)
+        multiply(2, 2)
+        nc.scalar.activation(y[:, 0:H], sums[0][:], IDENTITY, bias=bias[:])
+        nc.scalar.activation(y[:, H : H + P], sums[1][:], IDENTITY, bias=bias[:])
+        nc.vector.tensor_scalar_add(y[:, H + P : T], sums[2][:], bias[:])
+
+        terms = keep.tile([P, D, V], F32)
+        pairs = keep.tile([P, 2, V], F32)
+        even = keep.tile([P, V], F32)
+        odd = keep.tile([P, V], F32)
+        result = keep.tile([P, V], F32)
+        for d in range(D):
+            nc.vector.tensor_tensor(terms[:, d, :], y[:].indirect(offs[d][:]), gates[:, d, :], MULT)
+            if d == 4:
+                nc.vector.tensor_add(pairs[:], terms[:, 0:2, :], terms[:, 2:4, :])
+        nc.vector.tensor_add(even[:], pairs[:, 0, :], terms[:, 4, :])
+        halves = (slice(0, V // 2), slice(V // 2, V))
+        for c in halves:
+            nc.vector.tensor_add(odd[:, c], pairs[:, 1, c], terms[:, 5, c])
+        for c in halves:
+            nc.vector.tensor_add(result[:, c], even[:, c], odd[:, c])
+        nc.sync.dma_start(out=out, in_=result[:])

@@ -1,6 +1,7 @@
 from contextlib import ExitStack
 
 import concourse.mybir as mybir
+from concourse.masks import make_identity
 
 K, T, N, V, D = 1536, 512, 128, 256, 6
 FLOPS = 2 * K * T * N + 2 * D * N * V + T * N
@@ -30,32 +31,38 @@ def tile_picked_agg_lin_bias_sub_l_kernel(tc, xT, w_words, w_scales, b, gate, po
         psum = ctx.enter_context(tc.psum_pool(name="psum", bufs=1))
 
         offs = [lists.tile([P, V // 16], U16, name="offs%d" % d) for d in range(D)]
+        poss = (pos1, pos2, pos3, pos4, pos5, pos6)
         bias = keep.tile([P, 1], F32)
         w_codes = keep.tile([P, PASSES, N], U32, align_bytes=64)
         w_planes = keep.tile([P, PASSES, N], U8, align_bytes=64)
         warm = keep.tile([P, 2], F32)
         gates = keep.tile([P, D, V], F32)
-        x_codes = keep.tile([P, PASSES, T], U32, align_bytes=64)
-        x_scales = keep.tile([P, PASSES, T], U8, align_bytes=64)
         y = keep.tile([P, T], F32)
 
-        chunks = [(0, 0, T), (1, 0, T), (2, 0, H + P), (2, H + P, T)]
-        raws = [keep.tile([P, PACK, c1 - c0], F32, name="raw%d" % i) for i, (a, c0, c1) in enumerate(chunks)]
-        grouped = [keep.tile([P, c1 - c0, PACK], BF16, name="grouped%d" % i, align_bytes=64) for i, (a, c0, c1) in enumerate(chunks)]
+        chunks = [(0, 0, 512, 288), (1, 0, 512, 288), (2, 0, 256, 160), (2, 256, 384, 336), (2, 384, 512, 464)]
+        raws = [keep.tile([P, PACK, c1 - c0], F32, name="raw%d" % i) for i, (a, c0, c1, cs) in enumerate(chunks)]
+        grouped = [keep.tile([P, c1 - c0, PACK], BF16, name="grouped%d" % i, align_bytes=64) for i, (a, c0, c1, cs) in enumerate(chunks)]
+        groups = [(0, 256), (256, 384), (384, 512)]
+        sums = [psum.tile([P, t1 - t0], F32, name="sums%d" % g) for g, (t0, t1) in enumerate(groups)]
 
         def load(i):
-            a, c0, c1 = chunks[i]
+            a, c0, c1, cs = chunks[i]
             nc.sync.dma_start(out=raws[i][:], in_=xT[a * K_PASS : (a + 1) * K_PASS, c0:c1].rearrange("(p j) t -> p j t", j=PACK))
 
-        for q in range(4):
-            nc.scalar.dma_start(out=w_planes[32 * q : 32 * q + 4, :, :].bitcast(I32), in_=w_scales[:, 4 * q : 4 * q + 4, :].rearrange("a q m -> q a m").bitcast(I32))
+        def load_scales(queue):
+            for q in range(4):
+                queue.dma_start(out=w_planes[32 * q : 32 * q + 4, :, :].bitcast(I32), in_=w_scales[:, 4 * q : 4 * q + 4, :].rearrange("a q m -> q a m").bitcast(I32))
+
+        def load_words():
+            nc.sync.dma_start(out=w_codes[:].rearrange("p a m -> p (a m)").bitcast(I32).rearrange("p (a m) -> p a m", a=PASSES), in_=w_words.rearrange("a p m r -> p a (m r)").bitcast(I32))
+
+        load_scales(nc.scalar)
         nc.scalar.dma_start(out=bias[:], in_=b)
         load(0)
-        nc.sync.dma_start(out=w_codes[:].rearrange("p a m -> p (a m)").bitcast(I32).rearrange("p (a m) -> p a m", a=PASSES), in_=w_words.rearrange("a p m r -> p a (m r)").bitcast(I32))
         load(1)
-        load(2)
-        load(3)
-        poss = (pos1, pos2, pos3, pos4, pos5, pos6)
+        load_words()
+        for i in range(2, len(chunks)):
+            load(i)
         nc.sync.dma_start(offs[0][:], poss[0])
         nc.sync.dma_start(out=gates[:, 0:2, :], in_=gate[0:2].rearrange("d p v -> p d v"))
         nc.sync.dma_start(offs[1][:], poss[1])
@@ -69,63 +76,72 @@ def tile_picked_agg_lin_bias_sub_l_kernel(tc, xT, w_words, w_scales, b, gate, po
             c0 = chunks[i][1]
             copy(out=grouped[i][:, t0 - c0 : t1 - c0, :], in_=raws[i][:, :, t0 - c0 : t1 - c0].rearrange("p j t -> p t j"))
 
+        def spread(i):
+            a, c0, c1, cs = chunks[i]
+            if cs < c1:
+                interleave(nc.scalar.copy, i, cs, c1)
+            if c0 < cs:
+                interleave(nc.vector.tensor_copy, i, c0, cs)
+
         def quantize(i, t0, t1):
-            a, c0, c1 = chunks[i]
-            nc.vector.quantize_mx(
-                out=x_codes[:, a, t0:t1].bitcast(FP8X4),
-                scales=x_scales[:, a, t0:t1],
-                in_=grouped[i][:, t0 - c0 : t1 - c0, :].rearrange("p t j -> p (t j)"),
-            )
+            a, c0, c1, cs = chunks[i]
+            codes = keep.tile([P, t1 - t0], U32, name="codes%d_%d" % (a, t0), align_bytes=64)
+            scales = keep.tile([P, t1 - t0], U8, name="scales%d_%d" % (a, t0), align_bytes=64)
+            nc.vector.quantize_mx(out=codes[:].bitcast(FP8X4), scales=scales[:], in_=grouped[i][:, t0 - c0 : t1 - c0, :].rearrange("p t j -> p (t j)"))
+            for g, (g0, g1) in enumerate(groups):
+                if t0 <= g0 and g1 <= t1:
+                    nc.tensor.matmul_mx(
+                        out=sums[g][:],
+                        lhsT=w_codes[:, a, :].bitcast(FP8X4),
+                        lhsT_scale=w_planes[:, a, :],
+                        rhs=codes[:, g0 - t0 : g1 - t0].bitcast(FP8X4),
+                        rhs_scale=scales[:, g0 - t0 : g1 - t0],
+                        start=(a == 0),
+                        stop=(a == PASSES - 1),
+                    )
 
-        groups = [(0, H), (H, H + P), (H + P, T)]
-        sums = [psum.tile([P, t1 - t0], F32, name="sums%d" % g) for g, (t0, t1) in enumerate(groups)]
-
-        def multiply(a, g):
+        def empty_on_scalar(g):
             t0, t1 = groups[g]
-            nc.tensor.matmul_mx(
-                out=sums[g][:],
-                lhsT=w_codes[:, a, :].bitcast(FP8X4),
-                lhsT_scale=w_planes[:, a, :],
-                rhs=x_codes[:, a, t0:t1].bitcast(FP8X4),
-                rhs_scale=x_scales[:, a, t0:t1],
-                start=(a == 0),
-                stop=(a == PASSES - 1),
-            )
+            nc.scalar.activation(y[:, t0:t1], sums[g][:], IDENTITY, bias=bias[:])
 
-        for a in range(2):
-            interleave(nc.scalar.copy, a, H, T)
-            interleave(nc.vector.tensor_copy, a, 0, H)
-            quantize(a, 0, H)
-            quantize(a, H, T)
-            for g in range(3):
-                multiply(a, g)
-        interleave(nc.scalar.copy, 2, H, H + P)
-        interleave(nc.vector.tensor_copy, 2, 0, H)
-        quantize(2, 0, H)
-        quantize(2, H, H + P)
-        multiply(2, 0)
-        multiply(2, 1)
-        interleave(nc.scalar.copy, 3, T - 48, T)
-        interleave(nc.vector.tensor_copy, 3, H + P, T - 48)
-        quantize(3, H + P, T)
-        multiply(2, 2)
-        nc.scalar.activation(y[:, 0:H], sums[0][:], IDENTITY, bias=bias[:])
-        nc.scalar.activation(y[:, H : H + P], sums[1][:], IDENTITY, bias=bias[:])
-        nc.vector.tensor_scalar_add(y[:, H + P : T], sums[2][:], bias[:])
+        def empty_on_vector(g):
+            t0, t1 = groups[g]
+            nc.vector.tensor_scalar_add(y[:, t0:t1], sums[g][:], bias[:])
 
-        terms = keep.tile([P, D, V], F32)
-        pairs = keep.tile([P, 2, V], F32)
-        even = keep.tile([P, V], F32)
-        odd = keep.tile([P, V], F32)
-        result = keep.tile([P, V], F32)
-        for d in range(D):
-            nc.vector.tensor_tensor(terms[:, d, :], y[:].indirect(offs[d][:]), gates[:, d, :], MULT)
-            if d == 4:
-                nc.vector.tensor_add(pairs[:], terms[:, 0:2, :], terms[:, 2:4, :])
-        nc.vector.tensor_add(even[:], pairs[:, 0, :], terms[:, 4, :])
+        for i in range(2):
+            spread(i)
+            quantize(i, 0, H)
+            quantize(i, H, T)
+        for i in range(2, 5):
+            spread(i)
+            quantize(i, chunks[i][1], chunks[i][2])
+        empty_on_scalar(0)
+        empty_on_scalar(1)
+        empty_on_vector(2)
+
+        ident = keep.tile([P, P], F32)
+        make_identity(nc, ident[:])
         halves = (slice(0, V // 2), slice(V // 2, V))
+        terms = [keep.tile([P, V], F32, name="term%d" % d) for d in range(D)]
+        turned = [psum.tile([P, P], F32, name="turned%d" % h) for h in range(2)]
+        back = [psum.tile([P, P], F32, name="back%d" % h) for h in range(2)]
+        staged = [keep.tile([P, P], F32, name="staged%d" % h) for h in range(2)]
+        pair = keep.tile([P, V], F32)
+        result = keep.tile([P, V], F32)
+
+        ON_TENSOR = 4
+        for d in range(D):
+            nc.vector.tensor_tensor(terms[d][:], y[:].indirect(offs[d][:]), gates[:, d, :], MULT)
+            if d < ON_TENSOR:
+                for h in range(2):
+                    nc.tensor.matmul(turned[h][:], terms[d][:, halves[h]], ident[:], start=(d == 0), stop=(d == ON_TENSOR - 1), is_transpose=True)
+            if d == ON_TENSOR - 1:
+                for h in range(2):
+                    nc.scalar.copy(out=staged[h][:], in_=turned[h][:])
+                for h in range(2):
+                    nc.tensor.transpose(back[h][:], staged[h][:], ident[:])
         for c in halves:
-            nc.vector.tensor_add(odd[:, c], pairs[:, 1, c], terms[:, 5, c])
-        for c in halves:
-            nc.vector.tensor_add(result[:, c], even[:, c], odd[:, c])
+            nc.vector.tensor_add(pair[:, c], terms[4][:, c], terms[5][:, c])
+        for h in range(2):
+            nc.vector.tensor_add(result[:, halves[h]], back[h][:], pair[:, halves[h]])
         nc.sync.dma_start(out=out, in_=result[:])

@@ -37,10 +37,9 @@ def tile_picked_agg_lin_bias_sub_l_kernel(tc, xT, w_words, w_scales, b, gate, po
         w_planes = keep.tile([P, PASSES, N], U8, align_bytes=64)
         warm = keep.tile([P, 2], F32)
         gates = keep.tile([P, D, V], F32)
-        y = keep.tile([P, T], F32)
 
         chunks = [(0, 0, 512, 288), (1, 0, 512, 288), (2, 0, 256, 160), (2, 256, 384, 336), (2, 384, 512, 464)]
-        raws = [keep.tile([P, PACK, c1 - c0], F32, name="raw%d" % i) for i, (a, c0, c1, cs) in enumerate(chunks)]
+        raws = [keep.tile([P, PACK, c1 - c0], F32, name="raw%d" % i, tag="raw%d" % i) for i, (a, c0, c1, cs) in enumerate(chunks)]
         grouped = [keep.tile([P, c1 - c0, PACK], BF16, name="grouped%d" % i, align_bytes=64) for i, (a, c0, c1, cs) in enumerate(chunks)]
         groups = [(0, 256), (256, 384), (384, 512)]
         sums = [psum.tile([P, t1 - t0], F32, name="sums%d" % g) for g, (t0, t1) in enumerate(groups)]
@@ -57,12 +56,12 @@ def tile_picked_agg_lin_bias_sub_l_kernel(tc, xT, w_words, w_scales, b, gate, po
             nc.sync.dma_start(out=w_codes[:].rearrange("p a m -> p (a m)").bitcast(I32).rearrange("p (a m) -> p a m", a=PASSES), in_=w_words.rearrange("a p m r -> p a (m r)").bitcast(I32))
 
         load_scales(nc.scalar)
-        nc.scalar.dma_start(out=bias[:], in_=b)
         load(0)
         load(1)
         load_words()
         for i in range(2, len(chunks)):
             load(i)
+        nc.sync.dma_start(out=bias[:], in_=b)
         nc.sync.dma_start(offs[0][:], poss[0])
         nc.sync.dma_start(out=gates[:, 0:2, :], in_=gate[0:2].rearrange("d p v -> p d v"))
         nc.sync.dma_start(offs[1][:], poss[1])
@@ -100,11 +99,11 @@ def tile_picked_agg_lin_bias_sub_l_kernel(tc, xT, w_words, w_scales, b, gate, po
                         stop=(a == PASSES - 1),
                     )
 
-        def empty_on_scalar(g):
+        def empty_on_scalar(y, g):
             t0, t1 = groups[g]
             nc.scalar.activation(y[:, t0:t1], sums[g][:], IDENTITY, bias=bias[:])
 
-        def empty_on_vector(g):
+        def empty_on_vector(y, g):
             t0, t1 = groups[g]
             nc.vector.tensor_scalar_add(y[:, t0:t1], sums[g][:], bias[:])
 
@@ -115,9 +114,10 @@ def tile_picked_agg_lin_bias_sub_l_kernel(tc, xT, w_words, w_scales, b, gate, po
         for i in range(2, 5):
             spread(i)
             quantize(i, chunks[i][1], chunks[i][2])
-        empty_on_scalar(0)
-        empty_on_scalar(1)
-        empty_on_vector(2)
+        y = keep.tile([P, T], F32, tag="raw%d" % (len(chunks) - 1))
+        empty_on_scalar(y, 0)
+        empty_on_scalar(y, 1)
+        empty_on_vector(y, 2)
 
         ident = keep.tile([P, P], F32)
         make_identity(nc, ident[:])
@@ -126,11 +126,12 @@ def tile_picked_agg_lin_bias_sub_l_kernel(tc, xT, w_words, w_scales, b, gate, po
         turned = [psum.tile([P, P], F32, name="turned%d" % h) for h in range(2)]
         back = [psum.tile([P, P], F32, name="back%d" % h) for h in range(2)]
         staged = [keep.tile([P, P], F32, name="staged%d" % h) for h in range(2)]
-        pair = keep.tile([P, V], F32)
-        result = keep.tile([P, V], F32)
+        pair = [keep.tile([P, P], F32, name="pair%d" % h) for h in range(2)]
+        result = [keep.tile([P, P], F32, name="result%d" % h) for h in range(2)]
+        cols = V // 32
 
         ON_TENSOR = 4
-        for d in range(D):
+        for d in range(D - 1):
             nc.vector.tensor_tensor(terms[d][:], y[:].indirect(offs[d][:]), gates[:, d, :], MULT)
             if d < ON_TENSOR:
                 for h in range(2):
@@ -140,8 +141,11 @@ def tile_picked_agg_lin_bias_sub_l_kernel(tc, xT, w_words, w_scales, b, gate, po
                     nc.scalar.copy(out=staged[h][:], in_=turned[h][:])
                 for h in range(2):
                     nc.tensor.transpose(back[h][:], staged[h][:], ident[:])
-        for c in halves:
-            nc.vector.tensor_add(pair[:, c], terms[4][:, c], terms[5][:, c])
         for h in range(2):
-            nc.vector.tensor_add(result[:, halves[h]], back[h][:], pair[:, halves[h]])
-        nc.sync.dma_start(out=out, in_=result[:])
+            nc.vector.tensor_tensor(terms[D - 1][:, halves[h]], y[:].indirect(offs[D - 1][:, h * cols : (h + 1) * cols]), gates[:, D - 1, halves[h]], MULT)
+        for h in range(2):
+            nc.vector.tensor_add(pair[h][:], terms[D - 2][:, halves[h]], terms[D - 1][:, halves[h]])
+        for h in range(2):
+            nc.vector.tensor_add(result[h][:], back[h][:], pair[h][:])
+        for h, queue in enumerate((nc.sync, nc.scalar)):
+            queue.dma_start(out=out[:, halves[h]], in_=result[h][:])

@@ -32,7 +32,9 @@ def tile_picked_agg_lin_bias_sub_l_kernel(tc, xT, w_words, w_scales, b, gate, po
 
         offs = [lists.tile([P, V // 16], U16, name="offs%d" % d) for d in range(D)]
         poss = (pos1, pos2, pos3, pos4, pos5, pos6)
-        bias = keep.tile([P, 1], F32)
+        bias_rows = keep.tile([P, 32], F32, align_bytes=64)
+        bias_turned = keep.tile([P, 32], F32, align_bytes=64)
+        bias = bias_turned[:, 0:1]
         w_codes = keep.tile([P, PASSES, N], U32, align_bytes=64)
         w_planes = keep.tile([P, PASSES, N], U8, align_bytes=64)
         warm = keep.tile([P, 2], F32)
@@ -55,19 +57,19 @@ def tile_picked_agg_lin_bias_sub_l_kernel(tc, xT, w_words, w_scales, b, gate, po
         def load_words():
             nc.sync.dma_start(out=w_codes[:].rearrange("p a m -> p (a m)").bitcast(I32).rearrange("p (a m) -> p a m", a=PASSES), in_=w_words.rearrange("a p m r -> p a (m r)").bitcast(I32))
 
-        load_scales(nc.scalar)
+        nc.vector.memset(bias_rows[:], 0.0)
         load(0)
+        load_scales(nc.sync)
+        nc.sync.dma_start(out=bias_rows[0:P:32, :], in_=b.rearrange("(q i) o -> q (i o)", i=32))
+        nc.vector.transpose(bias_turned[:], bias_rows[:])
         load(1)
         load_words()
         for i in range(2, len(chunks)):
             load(i)
-        nc.sync.dma_start(out=bias[:], in_=b)
-        nc.sync.dma_start(offs[0][:], poss[0])
-        nc.sync.dma_start(out=gates[:, 0:2, :], in_=gate[0:2].rearrange("d p v -> p d v"))
-        nc.sync.dma_start(offs[1][:], poss[1])
-        nc.sync.dma_start(out=gates[:, 2:6, :], in_=gate[2:6].rearrange("d p v -> p d v"))
-        for d in range(2, 6):
+        for d in range(0, D, 2):
             nc.sync.dma_start(offs[d][:], poss[d])
+            nc.sync.dma_start(out=gates[:, d : d + 2, :], in_=gate[d : d + 2].rearrange("d p v -> p d v"))
+            nc.sync.dma_start(offs[d + 1][:], poss[d + 1])
         nc.vector.memset(warm[:], 0.0)
         nc.scalar.activation(warm[:, 0:1], warm[:, 1:2], IDENTITY)
 
@@ -101,11 +103,11 @@ def tile_picked_agg_lin_bias_sub_l_kernel(tc, xT, w_words, w_scales, b, gate, po
 
         def empty_on_scalar(y, g):
             t0, t1 = groups[g]
-            nc.scalar.activation(y[:, t0:t1], sums[g][:], IDENTITY, bias=bias[:])
+            nc.scalar.activation(y[:, t0:t1], sums[g][:], IDENTITY, bias=bias)
 
         def empty_on_vector(y, g):
             t0, t1 = groups[g]
-            nc.vector.tensor_scalar_add(y[:, t0:t1], sums[g][:], bias[:])
+            nc.vector.tensor_scalar_add(y[:, t0:t1], sums[g][:], bias)
 
         for i in range(2):
             spread(i)

@@ -118,8 +118,8 @@ def tile_picked_agg_lin_bias_sub_l_kernel(tc, xT, w_words, w_scales, b, gate, po
             quantize(i, chunks[i][1], chunks[i][2])
         y = keep.tile([P, T], F32, tag="raw%d" % (len(chunks) - 1))
         empty_on_scalar(y, 0)
-        empty_on_scalar(y, 1)
-        empty_on_vector(y, 2)
+        empty_on_vector(y, 1)
+        empty_on_scalar(y, 2)
 
         ident = keep.tile([P, P], F32)
         make_identity(nc, ident[:])

@@ -37,7 +37,6 @@ def tile_picked_agg_lin_bias_sub_l_kernel(tc, xT, w_words, w_scales, b, gate, po
         bias = bias_turned[:, 0:1]
         w_codes = keep.tile([P, PASSES, N], U32, align_bytes=64)
         w_planes = keep.tile([P, PASSES, N], U8, align_bytes=64)
-        warm = keep.tile([P, 2], F32)
         gates = keep.tile([P, D, V], F32)
 
         chunks = [(0, 0, 512, 288), (1, 0, 512, 288), (2, 0, 256, 160), (2, 256, 384, 336), (2, 384, 512, 464)]
@@ -70,8 +69,6 @@ def tile_picked_agg_lin_bias_sub_l_kernel(tc, xT, w_words, w_scales, b, gate, po
             nc.sync.dma_start(offs[d][:], poss[d])
             nc.sync.dma_start(out=gates[:, d : d + 2, :], in_=gate[d : d + 2].rearrange("d p v -> p d v"))
             nc.sync.dma_start(offs[d + 1][:], poss[d + 1])
-        nc.vector.memset(warm[:], 0.0)
-        nc.scalar.activation(warm[:, 0:1], warm[:, 1:2], IDENTITY)
 
         def interleave(copy, i, t0, t1):
             c0 = chunks[i][1]

@@ -32,9 +32,8 @@ def tile_picked_agg_lin_bias_sub_l_kernel(tc, xT, w_words, w_scales, b, gate, po
 
         offs = [lists.tile([P, V // 16], U16, name="offs%d" % d) for d in range(D)]
         poss = (pos1, pos2, pos3, pos4, pos5, pos6)
-        bias_rows = keep.tile([P, 32], F32, align_bytes=64)
-        bias_turned = keep.tile([P, 32], F32, align_bytes=64)
-        bias = bias_turned[:, 0:1]
+        bias_tile = keep.tile([P, 1], F32)
+        bias = bias_tile[:]
         w_codes = keep.tile([P, PASSES, N], U32, align_bytes=64)
         w_planes = keep.tile([P, PASSES, N], U8, align_bytes=64)
         gates = keep.tile([P, D, V], F32)
@@ -53,18 +52,17 @@ def tile_picked_agg_lin_bias_sub_l_kernel(tc, xT, w_words, w_scales, b, gate, po
             for q in range(4):
                 queue.dma_start(out=w_planes[32 * q : 32 * q + 4, :, :].bitcast(I32), in_=w_scales[:, 4 * q : 4 * q + 4, :].rearrange("a q m -> q a m").bitcast(I32))
 
-        def load_words():
-            nc.sync.dma_start(out=w_codes[:].rearrange("p a m -> p (a m)").bitcast(I32).rearrange("p (a m) -> p a m", a=PASSES), in_=w_words.rearrange("a p m r -> p a (m r)").bitcast(I32))
+        def load_words(a0, a1):
+            nc.sync.dma_start(out=w_codes[:, a0:a1, :].bitcast(I32), in_=w_words[a0:a1].rearrange("a p m r -> p a (m r)").bitcast(I32))
 
-        nc.vector.memset(bias_rows[:], 0.0)
         load(0)
         load_scales(nc.sync)
-        nc.sync.dma_start(out=bias_rows[0:P:32, :], in_=b.rearrange("(q i) o -> q (i o)", i=32))
-        nc.vector.transpose(bias_turned[:], bias_rows[:])
         load(1)
-        load_words()
+        load_words(0, PASSES - 1)
         for i in range(2, len(chunks)):
             load(i)
+        load_words(PASSES - 1, PASSES)
+        nc.sync.dma_start(out=bias, in_=b)
         for d in range(0, D, 2):
             nc.sync.dma_start(offs[d][:], poss[d])
             nc.sync.dma_start(out=gates[:, d : d + 2, :], in_=gate[d : d + 2].rearrange("d p v -> p d v"))

@@ -144,5 +144,5 @@ def tile_picked_agg_lin_bias_sub_l_kernel(tc, xT, w_words, w_scales, b, gate, po
             nc.vector.tensor_add(pair[h][:], terms[D - 2][:, halves[h]], terms[D - 1][:, halves[h]])
         for h in range(2):
             nc.vector.tensor_add(result[h][:], back[h][:], pair[h][:])
-        for h, queue in enumerate((nc.sync, nc.scalar)):
+        for h, queue in enumerate((nc.scalar, nc.scalar)):
             queue.dma_start(out=out[:, halves[h]], in_=result[h][:])

@@ -20,7 +20,9 @@ P = 128
 PACK = 4
 K_PASS = P * PACK
 PASSES = K // K_PASS
-H = T // 2
+LAST = PASSES - 1
+GROUPS = ((0, 256), (256, 384), (384, 512))
+ON_TENSOR = 4
 
 
 def tile_picked_agg_lin_bias_sub_l_kernel(tc, xT, w_words, w_scales, b, gate, pos1, pos2, pos3, pos4, pos5, pos6, out):
@@ -31,105 +33,102 @@ def tile_picked_agg_lin_bias_sub_l_kernel(tc, xT, w_words, w_scales, b, gate, po
         psum = ctx.enter_context(tc.psum_pool(name="psum", bufs=1))
 
         offs = [lists.tile([P, V // 16], U16, name="offs%d" % d) for d in range(D)]
-        poss = (pos1, pos2, pos3, pos4, pos5, pos6)
-        bias_tile = keep.tile([P, 1], F32)
-        bias = bias_tile[:]
+        positions = (pos1, pos2, pos3, pos4, pos5, pos6)
+        bias = keep.tile([P, 1], F32, tag="bias")
         w_codes = keep.tile([P, PASSES, N], U32, align_bytes=64)
         w_planes = keep.tile([P, PASSES, N], U8, align_bytes=64)
-        gates = keep.tile([P, D, V], F32)
+        sums = [psum.tile([P, t1 - t0], F32, name="sums%d" % g) for g, (t0, t1) in enumerate(GROUPS)]
+        gates = {}
 
-        chunks = [(0, 0, 512, 288), (1, 0, 512, 288), (2, 0, 256, 160), (2, 256, 384, 336), (2, 384, 512, 464)]
-        raws = [keep.tile([P, PACK, c1 - c0], F32, name="raw%d" % i, tag="raw%d" % i) for i, (a, c0, c1, cs) in enumerate(chunks)]
-        grouped = [keep.tile([P, c1 - c0, PACK], BF16, name="grouped%d" % i, align_bytes=64) for i, (a, c0, c1, cs) in enumerate(chunks)]
-        groups = [(0, 256), (256, 384), (384, 512)]
-        sums = [psum.tile([P, t1 - t0], F32, name="sums%d" % g) for g, (t0, t1) in enumerate(groups)]
+        def load_x(a, t0, t1):
+            raw = keep.tile([P, PACK, t1 - t0], F32, name="raw%d_%d" % (a, t0), tag="raw%d_%d" % (a, t0))
+            nc.sync.dma_start(out=raw[:], in_=xT[a * K_PASS : (a + 1) * K_PASS, t0:t1].rearrange("(p j) t -> p j t", j=PACK))
+            return raw
 
-        def load(i):
-            a, c0, c1, cs = chunks[i]
-            nc.sync.dma_start(out=raws[i][:], in_=xT[a * K_PASS : (a + 1) * K_PASS, c0:c1].rearrange("(p j) t -> p j t", j=PACK))
-
-        def load_scales(queue):
+        def load_scales():
             for q in range(4):
-                queue.dma_start(out=w_planes[32 * q : 32 * q + 4, :, :].bitcast(I32), in_=w_scales[:, 4 * q : 4 * q + 4, :].rearrange("a q m -> q a m").bitcast(I32))
+                nc.sync.dma_start(out=w_planes[32 * q : 32 * q + 4, :, :].bitcast(I32), in_=w_scales[:, 4 * q : 4 * q + 4, :].rearrange("a q m -> q a m").bitcast(I32))
 
         def load_words(a0, a1):
             nc.sync.dma_start(out=w_codes[:, a0:a1, :].bitcast(I32), in_=w_words[a0:a1].rearrange("a p m r -> p a (m r)").bitcast(I32))
 
-        load(0)
-        load_scales(nc.sync)
-        load(1)
-        load_words(0, PASSES - 1)
-        for i in range(2, len(chunks)):
-            load(i)
-        load_words(PASSES - 1, PASSES)
-        nc.sync.dma_start(out=bias, in_=b)
-        for d in range(0, D, 2):
-            nc.sync.dma_start(offs[d][:], poss[d])
-            nc.sync.dma_start(out=gates[:, d : d + 2, :], in_=gate[d : d + 2].rearrange("d p v -> p d v"))
-            nc.sync.dma_start(offs[d + 1][:], poss[d + 1])
+        def load_gates(queue, d0, d1, tag):
+            held = keep.tile([P, d1 - d0, V], F32, name="gates%d" % d0, tag=tag)
+            queue.dma_start(out=held[:], in_=gate[d0:d1].rearrange("d p v -> p d v"))
+            for d in range(d0, d1):
+                gates[d] = held[:, d - d0, :]
 
-        def interleave(copy, i, t0, t1):
-            c0 = chunks[i][1]
-            copy(out=grouped[i][:, t0 - c0 : t1 - c0, :], in_=raws[i][:, :, t0 - c0 : t1 - c0].rearrange("p j t -> p t j"))
+        raws = {}
+        raws[(0, 0)] = load_x(0, 0, 512)
+        raws[(1, 0)] = load_x(1, 0, 512)
+        raws[(2, 0)] = load_x(2, 0, 384)
+        load_scales()
+        load_words(0, 2)
+        raws[(2, 384)] = load_x(2, 384, 512)
+        load_words(LAST, PASSES)
+        nc.sync.dma_start(out=bias[:], in_=b)
+        nc.sync.dma_start(offs[0][:], positions[0])
+        load_gates(nc.sync, 0, 2, "gates0")
+        nc.sync.dma_start(offs[1][:], positions[1])
+        nc.sync.dma_start(offs[2][:], positions[2])
+        load_gates(nc.sync, 2, 4, "gates2")
+        nc.sync.dma_start(offs[3][:], positions[3])
+        nc.sync.dma_start(offs[4][:], positions[4])
+        load_gates(nc.sync, 4, 5, "gates4")
+        nc.sync.dma_start(offs[5][:], positions[5])
 
-        def spread(i):
-            a, c0, c1, cs = chunks[i]
-            if cs < c1:
-                interleave(nc.scalar.copy, i, cs, c1)
-            if c0 < cs:
-                interleave(nc.vector.tensor_copy, i, c0, cs)
+        def project(a, t0, t1, on_vector):
+            c0 = max(c for (pa, c) in raws if pa == a and c <= t0)
+            raw = raws[(a, c0)]
+            width = t1 - t0
+            grouped = keep.tile([P, width, PACK], BF16, name="grouped%d_%d" % (a, t0), align_bytes=64)
+            turned_view = raw[:, :, t0 - c0 : t1 - c0].rearrange("p j t -> p t j")
+            nc.scalar.copy(out=grouped[:, on_vector:, :], in_=turned_view[:, on_vector:, :])
+            nc.vector.tensor_copy(out=grouped[:, :on_vector, :], in_=turned_view[:, :on_vector, :])
+            for q0 in range(t0, t1, 256):
+                q1 = min(q0 + 256, t1)
+                codes = keep.tile([P, q1 - q0], U32, name="codes%d_%d" % (a, q0), align_bytes=64)
+                scales = keep.tile([P, q1 - q0], U8, name="scales%d_%d" % (a, q0), align_bytes=64)
+                nc.vector.quantize_mx(out=codes[:].bitcast(FP8X4), scales=scales[:], in_=grouped[:, q0 - t0 : q1 - t0, :].rearrange("p t j -> p (t j)"))
+                for g, (g0, g1) in enumerate(GROUPS):
+                    if q0 <= g0 and g1 <= q1:
+                        nc.tensor.matmul_mx(
+                            out=sums[g][:],
+                            lhsT=w_codes[:, a, :].bitcast(FP8X4),
+                            lhsT_scale=w_planes[:, a, :],
+                            rhs=codes[:, g0 - q0 : g1 - q0].bitcast(FP8X4),
+                            rhs_scale=scales[:, g0 - q0 : g1 - q0],
+                            start=(a == 0),
+                            stop=(a == LAST),
+                        )
 
-        def quantize(i, t0, t1):
-            a, c0, c1, cs = chunks[i]
-            codes = keep.tile([P, t1 - t0], U32, name="codes%d_%d" % (a, t0), align_bytes=64)
-            scales = keep.tile([P, t1 - t0], U8, name="scales%d_%d" % (a, t0), align_bytes=64)
-            nc.vector.quantize_mx(out=codes[:].bitcast(FP8X4), scales=scales[:], in_=grouped[i][:, t0 - c0 : t1 - c0, :].rearrange("p t j -> p (t j)"))
-            for g, (g0, g1) in enumerate(groups):
-                if t0 <= g0 and g1 <= t1:
-                    nc.tensor.matmul_mx(
-                        out=sums[g][:],
-                        lhsT=w_codes[:, a, :].bitcast(FP8X4),
-                        lhsT_scale=w_planes[:, a, :],
-                        rhs=codes[:, g0 - t0 : g1 - t0].bitcast(FP8X4),
-                        rhs_scale=scales[:, g0 - t0 : g1 - t0],
-                        start=(a == 0),
-                        stop=(a == PASSES - 1),
-                    )
+        project(0, 0, 512, 288)
+        project(1, 0, 512, 288)
+        project(2, 0, 256, 176)
+        project(2, 256, 384, 80)
+        project(2, 384, 512, 80)
 
-        def empty_on_scalar(y, g):
-            t0, t1 = groups[g]
-            nc.scalar.activation(y[:, t0:t1], sums[g][:], IDENTITY, bias=bias)
-
-        def empty_on_vector(y, g):
-            t0, t1 = groups[g]
-            nc.vector.tensor_scalar_add(y[:, t0:t1], sums[g][:], bias)
-
-        for i in range(2):
-            spread(i)
-            quantize(i, 0, H)
-            quantize(i, H, T)
-        for i in range(2, 5):
-            spread(i)
-            quantize(i, chunks[i][1], chunks[i][2])
-        y = keep.tile([P, T], F32, tag="raw%d" % (len(chunks) - 1))
-        empty_on_scalar(y, 0)
-        empty_on_vector(y, 1)
-        empty_on_scalar(y, 2)
+        y = keep.tile([P, T], F32, tag="raw%d_%d" % (LAST, GROUPS[-1][0]))
+        for g, (t0, t1) in enumerate(GROUPS):
+            if g in (0,):
+                nc.vector.tensor_scalar_add(y[:, t0:t1], sums[g][:], bias[:])
+            else:
+                nc.scalar.activation(y[:, t0:t1], sums[g][:], IDENTITY, bias=bias[:])
+        load_gates(nc.scalar, D - 1, D, "bias")
 
         ident = keep.tile([P, P], F32)
         make_identity(nc, ident[:])
         halves = (slice(0, V // 2), slice(V // 2, V))
+        cols = V // 32
         terms = [keep.tile([P, V], F32, name="term%d" % d) for d in range(D)]
         turned = [psum.tile([P, P], F32, name="turned%d" % h) for h in range(2)]
         back = [psum.tile([P, P], F32, name="back%d" % h) for h in range(2)]
         staged = [keep.tile([P, P], F32, name="staged%d" % h) for h in range(2)]
         pair = [keep.tile([P, P], F32, name="pair%d" % h) for h in range(2)]
         result = [keep.tile([P, P], F32, name="result%d" % h) for h in range(2)]
-        cols = V // 32
 
-        ON_TENSOR = 4
         for d in range(D - 1):
-            nc.vector.tensor_tensor(terms[d][:], y[:].indirect(offs[d][:]), gates[:, d, :], MULT)
+            nc.vector.tensor_tensor(terms[d][:], y[:].indirect(offs[d][:]), gates[d], MULT)
             if d < ON_TENSOR:
                 for h in range(2):
                     nc.tensor.matmul(turned[h][:], terms[d][:, halves[h]], ident[:], start=(d == 0), stop=(d == ON_TENSOR - 1), is_transpose=True)
@@ -139,10 +138,10 @@ def tile_picked_agg_lin_bias_sub_l_kernel(tc, xT, w_words, w_scales, b, gate, po
                 for h in range(2):
                     nc.tensor.transpose(back[h][:], staged[h][:], ident[:])
         for h in range(2):
-            nc.vector.tensor_tensor(terms[D - 1][:, halves[h]], y[:].indirect(offs[D - 1][:, h * cols : (h + 1) * cols]), gates[:, D - 1, halves[h]], MULT)
+            nc.vector.tensor_tensor(terms[D - 1][:, halves[h]], y[:].indirect(offs[D - 1][:, h * cols : (h + 1) * cols]), gates[D - 1][:, halves[h]], MULT)
         for h in range(2):
             nc.vector.tensor_add(pair[h][:], terms[D - 2][:, halves[h]], terms[D - 1][:, halves[h]])
         for h in range(2):
             nc.vector.tensor_add(result[h][:], back[h][:], pair[h][:])
-        for h, queue in enumerate((nc.scalar, nc.scalar)):
-            queue.dma_start(out=out[:, halves[h]], in_=result[h][:])
+        for h in range(2):
+            nc.scalar.dma_start(out=out[:, halves[h]], in_=result[h][:])

@@ -103,7 +103,8 @@ def tile_picked_agg_lin_bias_sub_l_kernel(tc, xT, w_words, w_scales, b, gate, po
                         )
 
         project(0, 0, 512, 288)
-        project(1, 0, 512, 288)
+        project(1, 0, 256, 160)
+        project(1, 256, 512, 160)
         project(2, 0, 256, 176)
         project(2, 256, 384, 80)
         project(2, 384, 512, 80)

@@ -14,6 +14,7 @@ U16 = mybir.dt.uint16
 U8 = mybir.dt.uint8
 FP8X4 = mybir.dt.float8_e4m3fn_x4
 IDENTITY = mybir.ActivationFunctionType.Identity
+COPY = mybir.ActivationFunctionType.Copy
 MULT = mybir.AluOpType.mult
 
 P = 128
@@ -22,7 +23,8 @@ K_PASS = P * PACK
 PASSES = K // K_PASS
 LAST = PASSES - 1
 GROUPS = ((0, 256), (256, 384), (384, 512))
-ON_TENSOR = 4
+ON_TENSOR = 2
+FUSED = 4
 
 
 def tile_picked_agg_lin_bias_sub_l_kernel(tc, xT, w_words, w_scales, b, gate, pos1, pos2, pos3, pos4, pos5, pos6, out):
@@ -37,7 +39,7 @@ def tile_picked_agg_lin_bias_sub_l_kernel(tc, xT, w_words, w_scales, b, gate, po
         bias = keep.tile([P, 1], F32, tag="bias")
         w_codes = keep.tile([P, PASSES, N], U32, align_bytes=64)
         w_planes = keep.tile([P, PASSES, N], U8, align_bytes=64)
-        sums = [psum.tile([P, t1 - t0], F32, name="sums%d" % g) for g, (t0, t1) in enumerate(GROUPS)]
+        sums = [psum.tile([P, t1 - t0], F32, name="sums%d" % g, tag="sums%d" % g) for g, (t0, t1) in enumerate(GROUPS)]
         gates = {}
 
         def load_x(a, t0, t1):
@@ -68,14 +70,18 @@ def tile_picked_agg_lin_bias_sub_l_kernel(tc, xT, w_words, w_scales, b, gate, po
         load_words(LAST, PASSES)
         nc.sync.dma_start(out=bias[:], in_=b)
         nc.sync.dma_start(offs[0][:], positions[0])
+        nc.sync.dma_start(offs[4][:], positions[4])
         load_gates(nc.sync, 0, 2, "gates0")
         nc.sync.dma_start(offs[1][:], positions[1])
+        nc.sync.dma_start(offs[5][:], positions[5])
         nc.sync.dma_start(offs[2][:], positions[2])
         load_gates(nc.sync, 2, 4, "gates2")
+        column_gates = keep.tile([P, 2 * (D - FUSED)], F32)
+        gate_halves = gate.rearrange("d m (h p) -> (d m h) p", p=P)
+        first = FUSED * 2 * N
+        with nc.allow_non_contiguous_dma(reason="one gate value a partition"):
+            nc.sync.dma_start(out=column_gates[:], in_=gate_halves[first : first + 3 * (N + 1) + 1 : N + 1, :].rearrange("j p -> p j"))
         nc.sync.dma_start(offs[3][:], positions[3])
-        nc.sync.dma_start(offs[4][:], positions[4])
-        load_gates(nc.sync, 4, 5, "gates4")
-        nc.sync.dma_start(offs[5][:], positions[5])
 
         def project(a, t0, t1, on_vector):
             c0 = max(c for (pa, c) in raws if pa == a and c <= t0)
@@ -115,33 +121,39 @@ def tile_picked_agg_lin_bias_sub_l_kernel(tc, xT, w_words, w_scales, b, gate, po
                 nc.vector.tensor_scalar_add(y[:, t0:t1], sums[g][:], bias[:])
             else:
                 nc.scalar.activation(y[:, t0:t1], sums[g][:], IDENTITY, bias=bias[:])
-        load_gates(nc.scalar, D - 1, D, "bias")
 
         ident = keep.tile([P, P], F32)
         make_identity(nc, ident[:])
         halves = (slice(0, V // 2), slice(V // 2, V))
         cols = V // 32
         terms = [keep.tile([P, V], F32, name="term%d" % d) for d in range(D)]
+        fetched = [psum.tile([P, V], F32, name="fetched%d" % d, tag="sums%d" % (d - FUSED)) for d in range(FUSED, D)]
         turned = [psum.tile([P, P], F32, name="turned%d" % h) for h in range(2)]
         back = [psum.tile([P, P], F32, name="back%d" % h) for h in range(2)]
+        scaled = [[keep.tile([P, P], F32, name="scaled%d_%d" % (d, h)) for h in range(2)] for d in range(FUSED, D)]
         staged = [keep.tile([P, P], F32, name="staged%d" % h) for h in range(2)]
         pair = [keep.tile([P, P], F32, name="pair%d" % h) for h in range(2)]
         result = [keep.tile([P, P], F32, name="result%d" % h) for h in range(2)]
 
-        for d in range(D - 1):
-            nc.vector.tensor_tensor(terms[d][:], y[:].indirect(offs[d][:]), gates[d], MULT)
-            if d < ON_TENSOR:
-                for h in range(2):
-                    nc.tensor.matmul(turned[h][:], terms[d][:, halves[h]], ident[:], start=(d == 0), stop=(d == ON_TENSOR - 1), is_transpose=True)
-            if d == ON_TENSOR - 1:
-                for h in range(2):
-                    nc.scalar.copy(out=staged[h][:], in_=turned[h][:])
-                for h in range(2):
-                    nc.tensor.transpose(back[h][:], staged[h][:], ident[:])
+        for i in range(ON_TENSOR):
+            nc.vector.tensor_tensor(terms[i][:], y[:].indirect(offs[i][:]), gates[i], MULT)
+            nc.scalar.activation(terms[FUSED + i][:], y[:].indirect(offs[FUSED + i][:]), COPY)
+            for h in range(2):
+                nc.tensor.matmul(turned[h][:], terms[i][:, halves[h]], ident[:], start=(i == 0), stop=(i == ON_TENSOR - 1), is_transpose=True)
+            for h in range(2):
+                nc.tensor.transpose(fetched[i][:, halves[h]], terms[FUSED + i][:, halves[h]], ident[:])
+        nc.vector.tensor_tensor(terms[2][:], y[:].indirect(offs[2][:]), gates[2], MULT)
         for h in range(2):
-            nc.vector.tensor_tensor(terms[D - 1][:, halves[h]], y[:].indirect(offs[D - 1][:, h * cols : (h + 1) * cols]), gates[D - 1][:, halves[h]], MULT)
+            nc.vector.tensor_tensor(terms[3][:, halves[h]], y[:].indirect(offs[3][:, h * cols : (h + 1) * cols]), gates[3][:, halves[h]], MULT)
         for h in range(2):
-            nc.vector.tensor_add(pair[h][:], terms[D - 2][:, halves[h]], terms[D - 1][:, halves[h]])
+            nc.scalar.activation(scaled[0][h][:], fetched[0][:, halves[h]], COPY, scale=column_gates[:, h : h + 1])
+        for h in range(2):
+            nc.scalar.copy(out=staged[h][:], in_=turned[h][:])
+            nc.scalar.activation(scaled[1][h][:], fetched[1][:, halves[h]], COPY, scale=column_gates[:, 2 + h : 3 + h])
+            for j, part in enumerate((scaled[0][h], staged[h], scaled[1][h])):
+                nc.tensor.matmul(back[h][:], part[:], ident[:], start=(j == 0), stop=(j == 2), is_transpose=True)
+        for h in range(2):
+            nc.vector.tensor_add(pair[h][:], terms[2][:, halves[h]], terms[3][:, halves[h]])
         for h in range(2):
             nc.vector.tensor_add(result[h][:], back[h][:], pair[h][:])
         for h in range(2):

@@ -55,11 +55,13 @@ def tile_picked_agg_lin_bias_sub_l_kernel(tc, xT, w_words, w_scales, b, gate, po
             nc.sync.dma_start(out=w_codes[:, a0:a1, :].bitcast(I32), in_=w_words[a0:a1].rearrange("a p m r -> p a (m r)").bitcast(I32))
 
         def load_gates(queue, d0, d1, tag):
-            held = keep.tile([P, d1 - d0, V], F32, name="gates%d" % d0, tag=tag)
+            held = keep.tile([P, d1 - d0, V], F32, name="gates%d" % d0, tag=tag, align_bytes=64)
             queue.dma_start(out=held[:], in_=gate[d0:d1].rearrange("d p v -> p d v"))
             for d in range(d0, d1):
                 gates[d] = held[:, d - d0, :]
 
+        rows = keep.tile([P, P], F32, align_bytes=64)
+        nc.vector.memset(rows[:], 0.0)
         raws = {}
         raws[(0, 0)] = load_x(0, 0, 512)
         raws[(1, 0)] = load_x(1, 0, 512)
@@ -74,13 +76,14 @@ def tile_picked_agg_lin_bias_sub_l_kernel(tc, xT, w_words, w_scales, b, gate, po
         load_gates(nc.sync, 0, 2, "gates0")
         nc.sync.dma_start(offs[1][:], positions[1])
         nc.sync.dma_start(offs[5][:], positions[5])
-        nc.sync.dma_start(offs[2][:], positions[2])
-        load_gates(nc.sync, 2, 4, "gates2")
-        column_gates = keep.tile([P, 2 * (D - FUSED)], F32)
         gate_halves = gate.rearrange("d m (h p) -> (d m h) p", p=P)
         first = FUSED * 2 * N
-        with nc.allow_non_contiguous_dma(reason="one gate value a partition"):
-            nc.sync.dma_start(out=column_gates[:], in_=gate_halves[first : first + 3 * (N + 1) + 1 : N + 1, :].rearrange("j p -> p j"))
+        nc.sync.dma_start(
+            out=rows[0:P:32, :].rearrange("q (j c) -> q j c", c=32),
+            in_=gate_halves[first : first + 3 * (N + 1) + 1 : N + 1, :].rearrange("j (q c) -> q j c", c=32),
+        )
+        nc.sync.dma_start(offs[2][:], positions[2])
+        load_gates(nc.sync, 2, 4, "gates2")
         nc.sync.dma_start(offs[3][:], positions[3])
 
         def project(a, t0, t1, on_vector):
@@ -137,6 +140,9 @@ def tile_picked_agg_lin_bias_sub_l_kernel(tc, xT, w_words, w_scales, b, gate, po
 
         for i in range(ON_TENSOR):
             nc.vector.tensor_tensor(terms[i][:], y[:].indirect(offs[i][:]), gates[i], MULT)
+            if i == 0:
+                columns = gates[0][:, :P]
+                nc.vector.transpose(columns, rows[:])
             nc.scalar.activation(terms[FUSED + i][:], y[:].indirect(offs[FUSED + i][:]), COPY)
             for h in range(2):
                 nc.tensor.matmul(turned[h][:], terms[i][:, halves[h]], ident[:], start=(i == 0), stop=(i == ON_TENSOR - 1), is_transpose=True)
@@ -146,10 +152,10 @@ def tile_picked_agg_lin_bias_sub_l_kernel(tc, xT, w_words, w_scales, b, gate, po
         for h in range(2):
             nc.vector.tensor_tensor(terms[3][:, halves[h]], y[:].indirect(offs[3][:, h * cols : (h + 1) * cols]), gates[3][:, halves[h]], MULT)
         for h in range(2):
-            nc.scalar.activation(scaled[0][h][:], fetched[0][:, halves[h]], COPY, scale=column_gates[:, h : h + 1])
+            nc.scalar.activation(scaled[0][h][:], fetched[0][:, halves[h]], COPY, scale=columns[:, 32 * h : 32 * h + 1])
         for h in range(2):
             nc.scalar.copy(out=staged[h][:], in_=turned[h][:])
-            nc.scalar.activation(scaled[1][h][:], fetched[1][:, halves[h]], COPY, scale=column_gates[:, 2 + h : 3 + h])
+            nc.scalar.activation(scaled[1][h][:], fetched[1][:, halves[h]], COPY, scale=columns[:, 64 + 32 * h : 65 + 32 * h])
             for j, part in enumerate((scaled[0][h], staged[h], scaled[1][h])):
                 nc.tensor.matmul(back[h][:], part[:], ident[:], start=(j == 0), stop=(j == 2), is_transpose=True)
         for h in range(2):

@@ -23,8 +23,8 @@ K_PASS = P * PACK
 PASSES = K // K_PASS
 LAST = PASSES - 1
 GROUPS = ((0, 256), (256, 384), (384, 512))
-ON_TENSOR = 2
-FUSED = 4
+SHARED = 4
+HALF = V // 2
 
 
 def tile_picked_agg_lin_bias_sub_l_kernel(tc, xT, w_words, w_scales, b, gate, pos1, pos2, pos3, pos4, pos5, pos6, out):
@@ -40,7 +40,6 @@ def tile_picked_agg_lin_bias_sub_l_kernel(tc, xT, w_words, w_scales, b, gate, po
         w_codes = keep.tile([P, PASSES, N], U32, align_bytes=64)
         w_planes = keep.tile([P, PASSES, N], U8, align_bytes=64)
         sums = [psum.tile([P, t1 - t0], F32, name="sums%d" % g, tag="sums%d" % g) for g, (t0, t1) in enumerate(GROUPS)]
-        gates = {}
 
         def load_x(a, t0, t1):
             raw = keep.tile([P, PACK, t1 - t0], F32, name="raw%d_%d" % (a, t0), tag="raw%d_%d" % (a, t0))
@@ -54,12 +53,6 @@ def tile_picked_agg_lin_bias_sub_l_kernel(tc, xT, w_words, w_scales, b, gate, po
         def load_words(a0, a1):
             nc.sync.dma_start(out=w_codes[:, a0:a1, :].bitcast(I32), in_=w_words[a0:a1].rearrange("a p m r -> p a (m r)").bitcast(I32))
 
-        def load_gates(queue, d0, d1, tag):
-            held = keep.tile([P, d1 - d0, V], F32, name="gates%d" % d0, tag=tag, align_bytes=64)
-            queue.dma_start(out=held[:], in_=gate[d0:d1].rearrange("d p v -> p d v"))
-            for d in range(d0, d1):
-                gates[d] = held[:, d - d0, :]
-
         rows = keep.tile([P, P], F32, align_bytes=64)
         nc.vector.memset(rows[:], 0.0)
         raws = {}
@@ -71,20 +64,16 @@ def tile_picked_agg_lin_bias_sub_l_kernel(tc, xT, w_words, w_scales, b, gate, po
         raws[(2, 384)] = load_x(2, 384, 512)
         load_words(LAST, PASSES)
         nc.sync.dma_start(out=bias[:], in_=b)
+        nc.sync.dma_start(out=rows[0:P:32, :].rearrange("q (d c) -> q d c", c=32), in_=gate[:SHARED, 0, HALF:].rearrange("d (q c) -> q d c", c=32))
         nc.sync.dma_start(offs[0][:], positions[0])
-        nc.sync.dma_start(offs[4][:], positions[4])
-        load_gates(nc.sync, 0, 2, "gates0")
-        nc.sync.dma_start(offs[1][:], positions[1])
-        nc.sync.dma_start(offs[5][:], positions[5])
-        gate_halves = gate.rearrange("d m (h p) -> (d m h) p", p=P)
-        first = FUSED * 2 * N
-        nc.sync.dma_start(
-            out=rows[0:P:32, :].rearrange("q (j c) -> q j c", c=32),
-            in_=gate_halves[first : first + 3 * (N + 1) + 1 : N + 1, :].rearrange("j (q c) -> q j c", c=32),
-        )
-        nc.sync.dma_start(offs[2][:], positions[2])
-        load_gates(nc.sync, 2, 4, "gates2")
-        nc.sync.dma_start(offs[3][:], positions[3])
+        low_gates = keep.tile([P, SHARED, HALF], F32, tag="low_gates", align_bytes=64)
+        nc.sync.dma_start(out=low_gates[:], in_=gate[:SHARED, :, :HALF].rearrange("d p v -> p d v"))
+        for d in range(1, SHARED):
+            nc.sync.dma_start(offs[d][:], positions[d])
+        last_gates = keep.tile([P, D - SHARED, V], F32, align_bytes=64)
+        nc.sync.dma_start(out=last_gates[:], in_=gate[SHARED:].rearrange("d p v -> p d v"))
+        for d in range(SHARED, D):
+            nc.sync.dma_start(offs[d][:], positions[d])
 
         def project(a, t0, t1, on_vector):
             c0 = max(c for (pa, c) in raws if pa == a and c <= t0)
@@ -96,7 +85,7 @@ def tile_picked_agg_lin_bias_sub_l_kernel(tc, xT, w_words, w_scales, b, gate, po
             nc.vector.tensor_copy(out=grouped[:, :on_vector, :], in_=turned_view[:, :on_vector, :])
             for q0 in range(t0, t1, 256):
                 q1 = min(q0 + 256, t1)
-                codes = keep.tile([P, q1 - q0], U32, name="codes%d_%d" % (a, q0), align_bytes=64)
+                codes = keep.tile([P, q1 - q0], U32, name="codes%d_%d" % (a, q0), tag="codes%d_%d" % (a, q0), align_bytes=64)
                 scales = keep.tile([P, q1 - q0], U8, name="scales%d_%d" % (a, q0), align_bytes=64)
                 nc.vector.quantize_mx(out=codes[:].bitcast(FP8X4), scales=scales[:], in_=grouped[:, q0 - t0 : q1 - t0, :].rearrange("p t j -> p (t j)"))
                 for g, (g0, g1) in enumerate(GROUPS):
@@ -125,42 +114,45 @@ def tile_picked_agg_lin_bias_sub_l_kernel(tc, xT, w_words, w_scales, b, gate, po
             else:
                 nc.scalar.activation(y[:, t0:t1], sums[g][:], IDENTITY, bias=bias[:])
 
+        columns = keep.tile([P, P], F32, tag="codes%d_0" % LAST, align_bytes=64)
+        nc.vector.transpose(columns[:], rows[:])
+
         ident = keep.tile([P, P], F32)
         make_identity(nc, ident[:])
-        halves = (slice(0, V // 2), slice(V // 2, V))
-        cols = V // 32
-        terms = [keep.tile([P, V], F32, name="term%d" % d) for d in range(D)]
-        fetched = [psum.tile([P, V], F32, name="fetched%d" % d, tag="sums%d" % (d - FUSED)) for d in range(FUSED, D)]
-        turned = [psum.tile([P, P], F32, name="turned%d" % h) for h in range(2)]
-        back = [psum.tile([P, P], F32, name="back%d" % h) for h in range(2)]
-        scaled = [[keep.tile([P, P], F32, name="scaled%d_%d" % (d, h)) for h in range(2)] for d in range(FUSED, D)]
-        staged = [keep.tile([P, P], F32, name="staged%d" % h) for h in range(2)]
-        pair = [keep.tile([P, P], F32, name="pair%d" % h) for h in range(2)]
-        result = [keep.tile([P, P], F32, name="result%d" % h) for h in range(2)]
+        low, high = slice(0, HALF), slice(HALF, V)
+        cols = HALF // 16
+        low_terms = [keep.tile([P, HALF], F32, name="low_term%d" % d) for d in range(SHARED)]
+        picked = [keep.tile([P, HALF], F32, name="picked%d" % d) for d in range(SHARED)]
+        turned = [psum.tile([P, P], F32, name="turned%d" % d) for d in range(SHARED)]
+        low_turned = psum.tile([P, P], F32)
+        for d in range(SHARED):
+            nc.scalar.activation(picked[d][:], y[:].indirect(offs[d][:, cols:]), COPY)
+            nc.vector.tensor_tensor(low_terms[d][:], y[:].indirect(offs[d][:, :cols]), low_gates[:, d, :], MULT)
+            nc.tensor.transpose(turned[d][:], picked[d][:], ident[:])
+            nc.tensor.matmul(low_turned[:], low_terms[d][:], ident[:], start=(d == 0), stop=(d == SHARED - 1), is_transpose=True)
 
-        for i in range(ON_TENSOR):
-            nc.vector.tensor_tensor(terms[i][:], y[:].indirect(offs[i][:]), gates[i], MULT)
-            if i == 0:
-                columns = gates[0][:, :P]
-                nc.vector.transpose(columns, rows[:])
-            nc.scalar.activation(terms[FUSED + i][:], y[:].indirect(offs[FUSED + i][:]), COPY)
-            for h in range(2):
-                nc.tensor.matmul(turned[h][:], terms[i][:, halves[h]], ident[:], start=(i == 0), stop=(i == ON_TENSOR - 1), is_transpose=True)
-            for h in range(2):
-                nc.tensor.transpose(fetched[i][:, halves[h]], terms[FUSED + i][:, halves[h]], ident[:])
-        nc.vector.tensor_tensor(terms[2][:], y[:].indirect(offs[2][:]), gates[2], MULT)
-        for h in range(2):
-            nc.vector.tensor_tensor(terms[3][:, halves[h]], y[:].indirect(offs[3][:, h * cols : (h + 1) * cols]), gates[3][:, halves[h]], MULT)
-        for h in range(2):
-            nc.scalar.activation(scaled[0][h][:], fetched[0][:, halves[h]], COPY, scale=columns[:, 32 * h : 32 * h + 1])
-        for h in range(2):
-            nc.scalar.copy(out=staged[h][:], in_=turned[h][:])
-            nc.scalar.activation(scaled[1][h][:], fetched[1][:, halves[h]], COPY, scale=columns[:, 64 + 32 * h : 65 + 32 * h])
-            for j, part in enumerate((scaled[0][h], staged[h], scaled[1][h])):
-                nc.tensor.matmul(back[h][:], part[:], ident[:], start=(j == 0), stop=(j == 2), is_transpose=True)
-        for h in range(2):
-            nc.vector.tensor_add(pair[h][:], terms[2][:, halves[h]], terms[3][:, halves[h]])
-        for h in range(2):
-            nc.vector.tensor_add(result[h][:], back[h][:], pair[h][:])
-        for h in range(2):
-            nc.scalar.dma_start(out=out[:, halves[h]], in_=result[h][:])
+        fifth = keep.tile([P, V], F32)
+        sixth = keep.tile([P, V], F32)
+        nc.vector.tensor_tensor(fifth[:], y[:].indirect(offs[D - 2][:]), last_gates[:, 0, :], MULT)
+        nc.vector.tensor_tensor(sixth[:, high], y[:].indirect(offs[D - 1][:, cols:]), last_gates[:, 1, high], MULT)
+        nc.vector.tensor_tensor(sixth[:, low], y[:].indirect(offs[D - 1][:, :cols]), last_gates[:, 1, low], MULT)
+
+        scaled = keep.tile([P, SHARED, HALF], F32, tag="low_gates", align_bytes=64)
+        staged = keep.tile([P, HALF], F32)
+        high_back = psum.tile([P, P], F32, tag="sums0")
+        low_back = psum.tile([P, P], F32, tag="sums1")
+        for d in range(SHARED):
+            nc.scalar.activation(scaled[:, d, :], turned[d][:], COPY, scale=columns[:, 32 * d : 32 * d + 1])
+            nc.tensor.matmul(high_back[:], scaled[:, d, :], ident[:], start=(d == 0), stop=(d == SHARED - 1), is_transpose=True)
+        nc.scalar.copy(out=staged[:], in_=low_turned[:])
+        nc.tensor.transpose(low_back[:], staged[:], ident[:])
+
+        halves = ((high, high_back), (low, low_back))
+        pair = [keep.tile([P, HALF], F32, name="pair%d" % h) for h in range(2)]
+        result = [keep.tile([P, HALF], F32, name="result%d" % h) for h in range(2)]
+        for h, (part, back) in enumerate(halves):
+            nc.vector.tensor_add(pair[h][:], fifth[:, part], sixth[:, part])
+        for h, (part, back) in enumerate(halves):
+            nc.vector.tensor_add(result[h][:], back[:], pair[h][:])
+        for h, (part, back) in enumerate(halves):
+            nc.scalar.dma_start(out=out[:, part], in_=result[h][:])

@@ -65,15 +65,14 @@ def tile_picked_agg_lin_bias_sub_l_kernel(tc, xT, w_words, w_scales, b, gate, po
         load_words(LAST, PASSES)
         nc.sync.dma_start(out=bias[:], in_=b)
         nc.sync.dma_start(out=rows[0:P:32, :].rearrange("q (d c) -> q d c", c=32), in_=gate[:SHARED, 0, HALF:].rearrange("d (q c) -> q d c", c=32))
-        nc.sync.dma_start(offs[0][:], positions[0])
         low_gates = keep.tile([P, SHARED, HALF], F32, tag="low_gates", align_bytes=64)
         nc.sync.dma_start(out=low_gates[:], in_=gate[:SHARED, :, :HALF].rearrange("d p v -> p d v"))
-        for d in range(1, SHARED):
+        for d in range(SHARED):
             nc.sync.dma_start(offs[d][:], positions[d])
-        last_gates = keep.tile([P, D - SHARED, V], F32, align_bytes=64)
-        nc.sync.dma_start(out=last_gates[:], in_=gate[SHARED:].rearrange("d p v -> p d v"))
+        last_gates = [keep.tile([P, V], F32, name="last_gate%d" % d) for d in range(SHARED, D)]
         for d in range(SHARED, D):
             nc.sync.dma_start(offs[d][:], positions[d])
+            nc.sync.dma_start(out=last_gates[d - SHARED][:], in_=gate[d])
 
         def project(a, t0, t1, on_vector):
             c0 = max(c for (pa, c) in raws if pa == a and c <= t0)
@@ -133,9 +132,9 @@ def tile_picked_agg_lin_bias_sub_l_kernel(tc, xT, w_words, w_scales, b, gate, po
 
         fifth = keep.tile([P, V], F32)
         sixth = keep.tile([P, V], F32)
-        nc.vector.tensor_tensor(fifth[:], y[:].indirect(offs[D - 2][:]), last_gates[:, 0, :], MULT)
-        nc.vector.tensor_tensor(sixth[:, high], y[:].indirect(offs[D - 1][:, cols:]), last_gates[:, 1, high], MULT)
-        nc.vector.tensor_tensor(sixth[:, low], y[:].indirect(offs[D - 1][:, :cols]), last_gates[:, 1, low], MULT)
+        nc.vector.tensor_tensor(fifth[:], y[:].indirect(offs[D - 2][:]), last_gates[0][:], MULT)
+        nc.vector.tensor_tensor(sixth[:, low], y[:].indirect(offs[D - 1][:, :cols]), last_gates[1][:, low], MULT)
+        nc.vector.tensor_tensor(sixth[:, high], y[:].indirect(offs[D - 1][:, cols:]), last_gates[1][:, high], MULT)
 
         scaled = keep.tile([P, SHARED, HALF], F32, tag="low_gates", align_bytes=64)
         staged = keep.tile([P, HALF], F32)
@@ -150,8 +149,8 @@ def tile_picked_agg_lin_bias_sub_l_kernel(tc, xT, w_words, w_scales, b, gate, po
         halves = ((high, high_back), (low, low_back))
         pair = [keep.tile([P, HALF], F32, name="pair%d" % h) for h in range(2)]
         result = [keep.tile([P, HALF], F32, name="result%d" % h) for h in range(2)]
-        for h, (part, back) in enumerate(halves):
-            nc.vector.tensor_add(pair[h][:], fifth[:, part], sixth[:, part])
+        for h in (1, 0):
+            nc.vector.tensor_add(pair[h][:], fifth[:, halves[h][0]], sixth[:, halves[h][0]])
         for h, (part, back) in enumerate(halves):
             nc.vector.tensor_add(result[h][:], back[:], pair[h][:])
         for h, (part, back) in enumerate(halves):

@@ -58,10 +58,14 @@ def tile_picked_agg_lin_bias_sub_l_kernel(tc, xT, w_words, w_scales, b, gate, po
         raws = {}
         raws[(0, 0)] = load_x(0, 0, 512)
         raws[(1, 0)] = load_x(1, 0, 512)
-        raws[(2, 0)] = load_x(2, 0, 384)
         load_scales()
-        load_words(0, 2)
-        raws[(2, 384)] = load_x(2, 384, 512)
+        last_rows = xT[LAST * K_PASS :, :].rearrange("(p j) t -> p j t", j=PACK)
+        last_raw = keep.tile([P, PACK, T], F32, tag="last_raw")
+        raws[(LAST, 0)] = last_raw
+        nc.sync.dma_start(out=last_raw[:, :, :384], in_=last_rows[:, :, :384])
+        load_words(0, 1)
+        load_words(1, 2)
+        nc.sync.dma_start(out=last_raw[:, :, 384:], in_=last_rows[:, :, 384:])
         load_words(LAST, PASSES)
         nc.sync.dma_start(out=bias[:], in_=b)
         nc.sync.dma_start(out=rows[0:P:32, :].rearrange("q (d c) -> q d c", c=32), in_=gate[:SHARED, 0, HALF:].rearrange("d (q c) -> q d c", c=32))
@@ -74,39 +78,46 @@ def tile_picked_agg_lin_bias_sub_l_kernel(tc, xT, w_words, w_scales, b, gate, po
             nc.sync.dma_start(offs[d][:], positions[d])
             nc.sync.dma_start(out=last_gates[d - SHARED][:], in_=gate[d])
 
+        def interleave(engine_copy, grouped, g0, raw, t0, t1):
+            engine_copy(out=grouped[:, t0 - g0 : t1 - g0, :], in_=raw[:, :, t0:t1].rearrange("p j t -> p t j"))
+
+        def multiply(a, grouped, g0, q0, q1):
+            codes = keep.tile([P, q1 - q0], U32, name="codes%d_%d" % (a, q0), tag="codes%d_%d" % (a, q0), align_bytes=64)
+            scales = keep.tile([P, q1 - q0], U8, name="scales%d_%d" % (a, q0), align_bytes=64)
+            nc.vector.quantize_mx(out=codes[:].bitcast(FP8X4), scales=scales[:], in_=grouped[:, q0 - g0 : q1 - g0, :].rearrange("p t j -> p (t j)"))
+            for g, (t0, t1) in enumerate(GROUPS):
+                if q0 <= t0 and t1 <= q1:
+                    nc.tensor.matmul_mx(
+                        out=sums[g][:],
+                        lhsT=w_codes[:, a, :].bitcast(FP8X4),
+                        lhsT_scale=w_planes[:, a, :],
+                        rhs=codes[:, t0 - q0 : t1 - q0].bitcast(FP8X4),
+                        rhs_scale=scales[:, t0 - q0 : t1 - q0],
+                        start=(a == 0),
+                        stop=(a == LAST),
+                    )
+
         def project(a, t0, t1, on_vector):
-            c0 = max(c for (pa, c) in raws if pa == a and c <= t0)
-            raw = raws[(a, c0)]
-            width = t1 - t0
-            grouped = keep.tile([P, width, PACK], BF16, name="grouped%d_%d" % (a, t0), align_bytes=64)
-            turned_view = raw[:, :, t0 - c0 : t1 - c0].rearrange("p j t -> p t j")
-            nc.scalar.copy(out=grouped[:, on_vector:, :], in_=turned_view[:, on_vector:, :])
-            nc.vector.tensor_copy(out=grouped[:, :on_vector, :], in_=turned_view[:, :on_vector, :])
+            grouped = keep.tile([P, t1 - t0, PACK], BF16, name="grouped%d_%d" % (a, t0), tag="grouped%d_%d" % (a, t0), align_bytes=64)
+            interleave(nc.scalar.copy, grouped, t0, raws[(a, 0)], t0 + on_vector, t1)
+            interleave(nc.vector.tensor_copy, grouped, t0, raws[(a, 0)], t0, t0 + on_vector)
             for q0 in range(t0, t1, 256):
-                q1 = min(q0 + 256, t1)
-                codes = keep.tile([P, q1 - q0], U32, name="codes%d_%d" % (a, q0), tag="codes%d_%d" % (a, q0), align_bytes=64)
-                scales = keep.tile([P, q1 - q0], U8, name="scales%d_%d" % (a, q0), align_bytes=64)
-                nc.vector.quantize_mx(out=codes[:].bitcast(FP8X4), scales=scales[:], in_=grouped[:, q0 - t0 : q1 - t0, :].rearrange("p t j -> p (t j)"))
-                for g, (g0, g1) in enumerate(GROUPS):
-                    if q0 <= g0 and g1 <= q1:
-                        nc.tensor.matmul_mx(
-                            out=sums[g][:],
-                            lhsT=w_codes[:, a, :].bitcast(FP8X4),
-                            lhsT_scale=w_planes[:, a, :],
-                            rhs=codes[:, g0 - q0 : g1 - q0].bitcast(FP8X4),
-                            rhs_scale=scales[:, g0 - q0 : g1 - q0],
-                            start=(a == 0),
-                            stop=(a == LAST),
-                        )
+                multiply(a, grouped, t0, q0, min(q0 + 256, t1))
 
         project(0, 0, 512, 288)
         project(1, 0, 256, 160)
         project(1, 256, 512, 160)
-        project(2, 0, 256, 176)
-        project(2, 256, 384, 80)
-        project(2, 384, 512, 80)
+        project(LAST, 0, 256, 160)
+        grouped = keep.tile([P, 256, PACK], BF16, align_bytes=64)
+        interleave(nc.scalar.copy, grouped, 256, last_raw, 320, 376)
+        interleave(nc.vector.tensor_copy, grouped, 256, last_raw, 256, 320)
+        interleave(nc.scalar.copy, grouped, 256, last_raw, 376, 392)
+        interleave(nc.scalar.copy, grouped, 256, last_raw, 472, 512)
+        interleave(nc.vector.tensor_copy, grouped, 256, last_raw, 392, 472)
+        multiply(LAST, grouped, 256, 256, 384)
+        multiply(LAST, grouped, 256, 384, 512)
 
-        y = keep.tile([P, T], F32, tag="raw%d_%d" % (LAST, GROUPS[-1][0]))
+        y = keep.tile([P, T], F32, tag="last_raw")
         for g, (t0, t1) in enumerate(GROUPS):
             if g in (0,):
                 nc.vector.tensor_scalar_add(y[:, t0:t1], sums[g][:], bias[:])

@@ -59,13 +59,15 @@ def tile_picked_agg_lin_bias_sub_l_kernel(tc, xT, w_words, w_scales, b, gate, po
         raws[(0, 0)] = load_x(0, 0, 512)
         raws[(1, 0)] = load_x(1, 0, 512)
         load_scales()
-        last_rows = xT[LAST * K_PASS :, :].rearrange("(p j) t -> p j t", j=PACK)
+        last_rows = xT[LAST * K_PASS :, :].rearrange("(p j) t -> p (j t)", j=PACK)
         last_raw = keep.tile([P, PACK, T], F32, tag="last_raw")
         raws[(LAST, 0)] = last_raw
-        nc.sync.dma_start(out=last_raw[:, :, :384], in_=last_rows[:, :, :384])
+        last_run = last_raw[:].rearrange("p j t -> p (j t)")
+        held_back = PACK * T - 128
+        nc.sync.dma_start(out=last_run[:, :held_back], in_=last_rows[:, :held_back])
         load_words(0, 1)
         load_words(1, 2)
-        nc.sync.dma_start(out=last_raw[:, :, 384:], in_=last_rows[:, :, 384:])
+        nc.sync.dma_start(out=last_run[:, held_back:], in_=last_rows[:, held_back:])
         load_words(LAST, PASSES)
         nc.sync.dma_start(out=bias[:], in_=b)
         nc.sync.dma_start(out=rows[0:P:32, :].rearrange("q (d c) -> q d c", c=32), in_=gate[:SHARED, 0, HALF:].rearrange("d (q c) -> q d c", c=32))
@@ -117,7 +119,7 @@ def tile_picked_agg_lin_bias_sub_l_kernel(tc, xT, w_words, w_scales, b, gate, po
         multiply(LAST, grouped, 256, 256, 384)
         multiply(LAST, grouped, 256, 384, 512)
 
-        y = keep.tile([P, T], F32, tag="last_raw")
+        y = keep.tile([P, T], F32)
         for g, (t0, t1) in enumerate(GROUPS):
             if g in (0,):
                 nc.vector.tensor_scalar_add(y[:, t0:t1], sums[g][:], bias[:])

@@ -63,11 +63,11 @@ def tile_picked_agg_lin_bias_sub_l_kernel(tc, xT, w_words, w_scales, b, gate, po
         last_raw = keep.tile([P, PACK, T], F32, tag="last_raw")
         raws[(LAST, 0)] = last_raw
         last_run = last_raw[:].rearrange("p j t -> p (j t)")
-        held_back = PACK * T - 128
+        held_back = PACK * T - 256
         nc.sync.dma_start(out=last_run[:, :held_back], in_=last_rows[:, :held_back])
         load_words(0, 1)
-        load_words(1, 2)
         nc.sync.dma_start(out=last_run[:, held_back:], in_=last_rows[:, held_back:])
+        load_words(1, 2)
         load_words(LAST, PASSES)
         nc.sync.dma_start(out=bias[:], in_=b)
         nc.sync.dma_start(out=rows[0:P:32, :].rearrange("q (d c) -> q d c", c=32), in_=gate[:SHARED, 0, HALF:].rearrange("d (q c) -> q d c", c=32))
@@ -83,20 +83,21 @@ def tile_picked_agg_lin_bias_sub_l_kernel(tc, xT, w_words, w_scales, b, gate, po
         def interleave(engine_copy, grouped, g0, raw, t0, t1):
             engine_copy(out=grouped[:, t0 - g0 : t1 - g0, :], in_=raw[:, :, t0:t1].rearrange("p j t -> p t j"))
 
-        def multiply(a, grouped, g0, q0, q1):
+        def multiply(a, grouped, n0, q0, q1):
             codes = keep.tile([P, q1 - q0], U32, name="codes%d_%d" % (a, q0), tag="codes%d_%d" % (a, q0), align_bytes=64)
             scales = keep.tile([P, q1 - q0], U8, name="scales%d_%d" % (a, q0), align_bytes=64)
-            nc.vector.quantize_mx(out=codes[:].bitcast(FP8X4), scales=scales[:], in_=grouped[:, q0 - g0 : q1 - g0, :].rearrange("p t j -> p (t j)"))
-            for g, (t0, t1) in enumerate(GROUPS):
-                if q0 <= t0 and t1 <= q1:
+            nc.vector.quantize_mx(out=codes[:].bitcast(FP8X4), scales=scales[:], in_=grouped[:, q0 - n0 : q1 - n0, :].rearrange("p t j -> p (t j)"))
+            for g, (g0, g1) in enumerate(GROUPS):
+                t0, t1 = max(g0, q0), min(g1, q1)
+                if t0 < t1:
                     nc.tensor.matmul_mx(
-                        out=sums[g][:],
+                        out=sums[g][:, t0 - g0 : t1 - g0],
                         lhsT=w_codes[:, a, :].bitcast(FP8X4),
                         lhsT_scale=w_planes[:, a, :],
                         rhs=codes[:, t0 - q0 : t1 - q0].bitcast(FP8X4),
                         rhs_scale=scales[:, t0 - q0 : t1 - q0],
                         start=(a == 0),
-                        stop=(a == LAST),
+                        stop=(a == LAST and t1 == g1),
                     )
 
         def project(a, t0, t1, on_vector):
@@ -109,15 +110,17 @@ def tile_picked_agg_lin_bias_sub_l_kernel(tc, xT, w_words, w_scales, b, gate, po
         project(0, 0, 512, 288)
         project(1, 0, 256, 160)
         project(1, 256, 512, 160)
-        project(LAST, 0, 256, 160)
-        grouped = keep.tile([P, 256, PACK], BF16, align_bytes=64)
-        interleave(nc.scalar.copy, grouped, 256, last_raw, 320, 376)
-        interleave(nc.vector.tensor_copy, grouped, 256, last_raw, 256, 320)
-        interleave(nc.scalar.copy, grouped, 256, last_raw, 376, 392)
-        interleave(nc.scalar.copy, grouped, 256, last_raw, 472, 512)
-        interleave(nc.vector.tensor_copy, grouped, 256, last_raw, 392, 472)
-        multiply(LAST, grouped, 256, 256, 384)
-        multiply(LAST, grouped, 256, 384, 512)
+        grouped = keep.tile([P, T, PACK], BF16, align_bytes=64)
+        interleave(nc.scalar.copy, grouped, 0, last_raw, 80, 128)
+        interleave(nc.vector.tensor_copy, grouped, 0, last_raw, 0, 80)
+        interleave(nc.scalar.copy, grouped, 0, last_raw, 200, 248)
+        interleave(nc.vector.tensor_copy, grouped, 0, last_raw, 128, 200)
+        multiply(LAST, grouped, 0, 0, 128)
+        interleave(nc.scalar.copy, grouped, 0, last_raw, 248, 264)
+        interleave(nc.scalar.copy, grouped, 0, last_raw, 420, 512)
+        interleave(nc.vector.tensor_copy, grouped, 0, last_raw, 264, 420)
+        for t0 in (128, 256, 384):
+            multiply(LAST, grouped, 0, t0, t0 + 128)
 
         y = keep.tile([P, T], F32)
         for g, (t0, t1) in enumerate(GROUPS):
@@ -126,7 +129,7 @@ def tile_picked_agg_lin_bias_sub_l_kernel(tc, xT, w_words, w_scales, b, gate, po
             else:
                 nc.scalar.activation(y[:, t0:t1], sums[g][:], IDENTITY, bias=bias[:])
 
-        columns = keep.tile([P, P], F32, tag="codes%d_0" % LAST, align_bytes=64)
+        columns = keep.tile([P, P], F32, tag="codes%d_128" % LAST, align_bytes=64)
         nc.vector.transpose(columns[:], rows[:])
 
         ident = keep.tile([P, P], F32)

from contextlib import ExitStack

import concourse.mybir as mybir
from concourse.masks import make_identity

K, T, N, V, D = 1536, 512, 128, 256, 6
FLOPS = 2 * K * T * N + 2 * D * N * V + T * N

F32 = mybir.dt.float32
BF16 = mybir.dt.bfloat16
I32 = mybir.dt.int32
U32 = mybir.dt.uint32
U16 = mybir.dt.uint16
U8 = mybir.dt.uint8
FP8X4 = mybir.dt.float8_e4m3fn_x4
IDENTITY = mybir.ActivationFunctionType.Identity
COPY = mybir.ActivationFunctionType.Copy
MULT = mybir.AluOpType.mult

P = 128
PACK = 4
K_PASS = P * PACK
PASSES = K // K_PASS
LAST = PASSES - 1
GROUPS = ((0, 256), (256, 384), (384, 512))
SHARED = 4
HALF = V // 2


def tile_picked_agg_lin_bias_sub_l_kernel(tc, xT, w_words, w_scales, b, gate, pos1, pos2, pos3, pos4, pos5, pos6, out):
    nc = tc.nc
    with ExitStack() as ctx:
        lists = ctx.enter_context(tc.tile_pool(name="lists", bufs=1))
        keep = ctx.enter_context(tc.tile_pool(name="keep", bufs=1))
        psum = ctx.enter_context(tc.psum_pool(name="psum", bufs=1))

        offs = [lists.tile([P, V // 16], U16, name="offs%d" % d) for d in range(D)]
        positions = (pos1, pos2, pos3, pos4, pos5, pos6)
        bias = keep.tile([P, 1], F32, tag="bias")
        w_codes = keep.tile([P, PASSES, N], U32, align_bytes=64)
        w_planes = keep.tile([P, PASSES, N], U8, align_bytes=64)
        sums = [psum.tile([P, t1 - t0], F32, name="sums%d" % g, tag="sums%d" % g) for g, (t0, t1) in enumerate(GROUPS)]

        def load_x(a, t0, t1):
            raw = keep.tile([P, PACK, t1 - t0], F32, name="raw%d_%d" % (a, t0), tag="raw%d_%d" % (a, t0))
            nc.sync.dma_start(out=raw[:], in_=xT[a * K_PASS : (a + 1) * K_PASS, t0:t1].rearrange("(p j) t -> p j t", j=PACK))
            return raw

        def load_scales():
            for q in range(4):
                nc.sync.dma_start(out=w_planes[32 * q : 32 * q + 4, :, :].bitcast(I32), in_=w_scales[:, 4 * q : 4 * q + 4, :].rearrange("a q m -> q a m").bitcast(I32))

        def load_words(a0, a1):
            nc.sync.dma_start(out=w_codes[:, a0:a1, :].bitcast(I32), in_=w_words[a0:a1].rearrange("a p m r -> p a (m r)").bitcast(I32))

        rows = keep.tile([P, P], F32, align_bytes=64)
        nc.vector.memset(rows[:], 0.0)
        raws = {}
        raws[(0, 0)] = load_x(0, 0, 512)
        raws[(1, 0)] = load_x(1, 0, 512)
        load_scales()
        last_rows = xT[LAST * K_PASS :, :].rearrange("(p j) t -> p (j t)", j=PACK)
        last_raw = keep.tile([P, PACK, T], F32, tag="last_raw")
        raws[(LAST, 0)] = last_raw
        last_run = last_raw[:].rearrange("p j t -> p (j t)")
        held_back = PACK * T - 256
        nc.sync.dma_start(out=last_run[:, :held_back], in_=last_rows[:, :held_back])
        load_words(0, 1)
        nc.sync.dma_start(out=last_run[:, held_back:], in_=last_rows[:, held_back:])
        load_words(1, 2)
        load_words(LAST, PASSES)
        nc.sync.dma_start(out=bias[:], in_=b)
        nc.sync.dma_start(out=rows[0:P:32, :].rearrange("q (d c) -> q d c", c=32), in_=gate[:SHARED, 0, HALF:].rearrange("d (q c) -> q d c", c=32))
        low_gates = keep.tile([P, SHARED, HALF], F32, tag="low_gates", align_bytes=64)
        nc.sync.dma_start(out=low_gates[:], in_=gate[:SHARED, :, :HALF].rearrange("d p v -> p d v"))
        for d in range(SHARED):
            nc.sync.dma_start(offs[d][:], positions[d])
        last_gates = [keep.tile([P, V], F32, name="last_gate%d" % d) for d in range(SHARED, D)]
        for d in range(SHARED, D):
            nc.sync.dma_start(offs[d][:], positions[d])
            nc.sync.dma_start(out=last_gates[d - SHARED][:], in_=gate[d])

        def interleave(engine_copy, grouped, g0, raw, t0, t1):
            engine_copy(out=grouped[:, t0 - g0 : t1 - g0, :], in_=raw[:, :, t0:t1].rearrange("p j t -> p t j"))

        def multiply(a, grouped, n0, q0, q1):
            codes = keep.tile([P, q1 - q0], U32, name="codes%d_%d" % (a, q0), tag="codes%d_%d" % (a, q0), align_bytes=64)
            scales = keep.tile([P, q1 - q0], U8, name="scales%d_%d" % (a, q0), align_bytes=64)
            nc.vector.quantize_mx(out=codes[:].bitcast(FP8X4), scales=scales[:], in_=grouped[:, q0 - n0 : q1 - n0, :].rearrange("p t j -> p (t j)"))
            for g, (g0, g1) in enumerate(GROUPS):
                t0, t1 = max(g0, q0), min(g1, q1)
                if t0 < t1:
                    nc.tensor.matmul_mx(
                        out=sums[g][:, t0 - g0 : t1 - g0],
                        lhsT=w_codes[:, a, :].bitcast(FP8X4),
                        lhsT_scale=w_planes[:, a, :],
                        rhs=codes[:, t0 - q0 : t1 - q0].bitcast(FP8X4),
                        rhs_scale=scales[:, t0 - q0 : t1 - q0],
                        start=(a == 0),
                        stop=(a == LAST and t1 == g1),
                    )

        def project(a, t0, t1, on_vector):
            grouped = keep.tile([P, t1 - t0, PACK], BF16, name="grouped%d_%d" % (a, t0), tag="grouped%d_%d" % (a, t0), align_bytes=64)
            interleave(nc.scalar.copy, grouped, t0, raws[(a, 0)], t0 + on_vector, t1)
            interleave(nc.vector.tensor_copy, grouped, t0, raws[(a, 0)], t0, t0 + on_vector)
            for q0 in range(t0, t1, 256):
                multiply(a, grouped, t0, q0, min(q0 + 256, t1))

        project(0, 0, 512, 288)
        project(1, 0, 256, 160)
        project(1, 256, 512, 160)
        grouped = keep.tile([P, T, PACK], BF16, align_bytes=64)
        interleave(nc.scalar.copy, grouped, 0, last_raw, 80, 128)
        interleave(nc.vector.tensor_copy, grouped, 0, last_raw, 0, 80)
        interleave(nc.scalar.copy, grouped, 0, last_raw, 200, 248)
        interleave(nc.vector.tensor_copy, grouped, 0, last_raw, 128, 200)
        multiply(LAST, grouped, 0, 0, 128)
        interleave(nc.scalar.copy, grouped, 0, last_raw, 248, 264)
        interleave(nc.scalar.copy, grouped, 0, last_raw, 420, 512)
        interleave(nc.vector.tensor_copy, grouped, 0, last_raw, 264, 420)
        for t0 in (128, 256, 384):
            multiply(LAST, grouped, 0, t0, t0 + 128)

        y = keep.tile([P, T], F32)
        for g, (t0, t1) in enumerate(GROUPS):
            if g in (0,):
                nc.vector.tensor_scalar_add(y[:, t0:t1], sums[g][:], bias[:])
            else:
                nc.scalar.activation(y[:, t0:t1], sums[g][:], IDENTITY, bias=bias[:])

        columns = keep.tile([P, P], F32, tag="codes%d_128" % LAST, align_bytes=64)
        nc.vector.transpose(columns[:], rows[:])

        ident = keep.tile([P, P], F32)
        make_identity(nc, ident[:])
        low, high = slice(0, HALF), slice(HALF, V)
        cols = HALF // 16
        low_terms = [keep.tile([P, HALF], F32, name="low_term%d" % d) for d in range(SHARED)]
        picked = [keep.tile([P, HALF], F32, name="picked%d" % d) for d in range(SHARED)]
        turned = [psum.tile([P, P], F32, name="turned%d" % d) for d in range(SHARED)]
        low_turned = psum.tile([P, P], F32)
        for d in range(SHARED):
            nc.scalar.activation(picked[d][:], y[:].indirect(offs[d][:, cols:]), COPY)
            nc.vector.tensor_tensor(low_terms[d][:], y[:].indirect(offs[d][:, :cols]), low_gates[:, d, :], MULT)
            nc.tensor.transpose(turned[d][:], picked[d][:], ident[:])
            nc.tensor.matmul(low_turned[:], low_terms[d][:], ident[:], start=(d == 0), stop=(d == SHARED - 1), is_transpose=True)

        fifth = keep.tile([P, V], F32)
        sixth = keep.tile([P, V], F32)
        nc.vector.tensor_tensor(fifth[:], y[:].indirect(offs[D - 2][:]), last_gates[0][:], MULT)
        nc.vector.tensor_tensor(sixth[:, low], y[:].indirect(offs[D - 1][:, :cols]), last_gates[1][:, low], MULT)
        nc.vector.tensor_tensor(sixth[:, high], y[:].indirect(offs[D - 1][:, cols:]), last_gates[1][:, high], MULT)

        scaled = keep.tile([P, SHARED, HALF], F32, tag="low_gates", align_bytes=64)
        staged = keep.tile([P, HALF], F32)
        high_back = psum.tile([P, P], F32, tag="sums0")
        low_back = psum.tile([P, P], F32, tag="sums1")
        for d in range(SHARED):
            nc.scalar.activation(scaled[:, d, :], turned[d][:], COPY, scale=columns[:, 32 * d : 32 * d + 1])
            nc.tensor.matmul(high_back[:], scaled[:, d, :], ident[:], start=(d == 0), stop=(d == SHARED - 1), is_transpose=True)
        nc.scalar.copy(out=staged[:], in_=low_turned[:])
        nc.tensor.transpose(low_back[:], staged[:], ident[:])

        halves = ((high, high_back), (low, low_back))
        pair = [keep.tile([P, HALF], F32, name="pair%d" % h) for h in range(2)]
        result = [keep.tile([P, HALF], F32, name="result%d" % h) for h in range(2)]
        for h in (1, 0):
            nc.vector.tensor_add(pair[h][:], fifth[:, halves[h][0]], sixth[:, halves[h][0]])
        for h, (part, back) in enumerate(halves):
            nc.vector.tensor_add(result[h][:], back[:], pair[h][:])
        for h, (part, back) in enumerate(halves):
            nc.scalar.dma_start(out=out[:, part], in_=result[h][:])
